import numpy as np
import ml_dtypes


def mxq(x, axis, fmt="e4m3"):
    dtype, down = {"e4m3": (ml_dtypes.float8_e4m3fn, 7), "e5m2": (ml_dtypes.float8_e5m2, 14)}[fmt]
    v = np.moveaxis(np.asarray(x, np.float32).astype(ml_dtypes.bfloat16).astype(np.float64), axis, -1)
    blocks = v.reshape(v.shape[:-1] + (-1, 32))
    amax = np.abs(blocks).max(-1, keepdims=True)
    byte = np.maximum(np.where(amax > 0, np.frexp(amax)[1] - 1 + 127, 0) - down, 1)
    scale = np.exp2(byte - 127.0)
    codes = (blocks / scale).astype(np.float32).astype(dtype).astype(np.float64)
    return np.moveaxis((codes * scale).reshape(v.shape), -1, axis)


WIDE = False


def mx_kscale(k):
    if not WIDE:
        return np.ones(k)
    levels = np.array([10, -10, 5, -5, 0])
    if k % 512:
        return np.exp2(np.random.permutation(np.resize(levels, k // 32))).repeat(32)
    a = np.empty((k // 512, 16))
    for p in range(k // 512):
        a[p, :8] = np.random.permutation(np.resize(levels, 8))
        for g in range(8):
            far = levels[np.abs(levels - a[p, g]) >= 10]
            a[p, g + 8] = far[np.random.randint(len(far))]
    return np.exp2(a.ravel()).repeat(32)


def f64(x):
    return np.asarray(x).astype(np.float64)


def striped(idx):
    return np.tile(idx.reshape(-1, 16).T, (8, 1)).astype(np.uint16)


def unstriped(offs):
    return offs[:16].T.reshape(-1).astype(np.int64)


def striped8(idx):
    return np.concatenate([x.reshape(-1, 16).T for x in idx]).astype(np.uint16)


def runs(offs, k):
    lists = np.stack([offs[16 * r : 16 * r + 16].T.reshape(-1) for r in range(8)]).astype(np.int64)
    return lists[np.arange(k) % 512 // 64]


def pack_weight(w):
    k, n = w.shape
    w = f64(np.asarray(w, np.float32).astype(ml_dtypes.bfloat16)).reshape(k // 32, 32, n)
    amax = np.abs(w).max(1)
    byte = np.clip(np.where(amax > 0, np.frexp(amax)[1] - 1 + 127 - 7, 1), 1, 254)
    scaled = (w * np.exp2(127.0 - byte)[:, None, :]).reshape(k, n).astype(np.float32)
    words = np.ascontiguousarray(scaled.reshape(k // 512, 128, 4, n).transpose(0, 1, 3, 2)).astype(ml_dtypes.float8_e4m3fn).view(np.uint8)
    return words, np.ascontiguousarray(byte.astype(np.uint8).reshape(k // 512, 16, n))


def unpack_weight(words, scales):
    g, p, n, _ = words.shape
    vals = np.ascontiguousarray(words).view(ml_dtypes.float8_e4m3fn).astype(np.float64) * np.repeat(np.exp2(scales.astype(np.float64) - 127.0), 8, axis=1)[..., None]
    return vals.transpose(0, 1, 3, 2).reshape(g * 512, n)

def planes(y):
    n, m = y.shape
    v = y.astype(np.float32).astype(ml_dtypes.bfloat16).astype(np.float64).reshape(n // 32, 32, m)
    top = np.abs(v).max(1)
    byte = np.clip(np.where(top > 0, np.frexp(top)[1] - 1 + 127 - 7, 1), 1, 254)
    codes = (v * np.exp2(127.0 - byte)[:, None, :]).reshape(n, m).astype(np.float32).astype(ml_dtypes.float8_e4m3fn).view(np.uint8)
    words = codes.reshape(n // 512, 128, 4, m).transpose(0, 1, 3, 2)
    return np.ascontiguousarray(words), np.ascontiguousarray(byte.astype(np.uint8).reshape(n // 512, 16, m))


K, T, S, N, H = 512, 2048, 256, 512, 512


def setup_inputs():
    n = np.random.standard_normal
    s = mx_kscale(K)[:, None]
    u = mx_kscale(H)
    packed_xT = pack_weight(n((K, T)) * s)
    packed_w1 = pack_weight(n((K, H)) / np.sqrt(K) / s)
    packed_w2 = pack_weight(n((K, H)) / np.sqrt(K) / s)
    packed_w3 = pack_weight(n((H, N)) / np.sqrt(2 * H) / u[:, None])
    packed_w4 = pack_weight(n((H, N)) / np.sqrt(2 * H) / u[:, None])
    return {
        "x_words": packed_xT[0],
        "x_scales": packed_xT[1],
        "w1_words": packed_w1[0],
        "w1_scales": packed_w1[1],
        "w2_words": packed_w2[0],
        "w2_scales": packed_w2[1],
        "gn": (np.random.uniform(0.5, 1.5, (H, 1)) * u[:, None]).astype(np.float32),
        "gm": (np.random.uniform(0.5, 1.5, (H, 1)) * u[:, None]).astype(np.float32),
        "w3_words": packed_w3[0],
        "w3_scales": packed_w3[1],
        "w4_words": packed_w4[0],
        "w4_scales": packed_w4[1],
        "offs": striped(np.random.permutation(T)[:S]),
        "hz": striped8(np.random.randint(0, T, (8, S))),
        "n1": striped(np.random.permutation(S)),
        "n2": striped(np.random.permutation(S)),
        "n3": striped8(np.stack([np.random.permutation(S) for _ in range(8)])),
        "n4": striped8(np.stack([np.random.permutation(S) for _ in range(8)])),
        "n5": striped8(np.stack([np.random.permutation(S) for _ in range(8)])),
        "n6": striped8(np.stack([np.random.permutation(S) for _ in range(8)])),
        "n7": striped8(np.stack([np.random.permutation(S) for _ in range(8)])),
    }


def reference(x_words, x_scales, w1_words, w1_scales, w2_words, w2_scales, gn, gm, w3_words, w3_scales, w4_words, w4_scales, offs, hz, n1, n2, n3, n4, n5, n6, n7):
    xq = unpack_weight(x_words, x_scales)[:, unstriped(offs)]
    y = unpack_weight(w1_words, w1_scales).T @ xq
    pa = y[:, unstriped(n1)]
    pb = y[:, unstriped(n2)]
    z = f64(gn) * (np.maximum(np.minimum(y, pa), np.minimum(np.maximum(y, pa), pb)))
    x_hz = unpack_weight(x_words, x_scales)[np.arange(K)[:, None], runs(hz, K)]
    d = unpack_weight(w2_words, w2_scales).T @ x_hz
    z2 = f64(gm) * (d * (d[np.arange(H)[:, None], runs(n3, H)] - (d[np.arange(H)[:, None], runs(n4, H)])))
    h = unpack_weight(w3_words, w3_scales).T @ mxq(z, 0, "e4m3") + unpack_weight(w4_words, w4_scales).T @ mxq(z2, 0, "e4m3")
    b1 = h[np.arange(N)[:, None], runs(n5, N)]
    b2 = h[np.arange(N)[:, None], runs(n6, N)]
    b3 = h[np.arange(N)[:, None], runs(n7, N)]
    out_0 = np.maximum(np.maximum(b1, b2), b3) - (0.5 * (np.maximum(np.minimum(b1, b2), np.minimum(np.maximum(b1, b2), b3))))
    return (out_0,) + planes(out_0)

@@ -1,0 +1,230 @@
+from contextlib import ExitStack
+
+import concourse.mybir as mybir
+
+K, T, S, N, H = 512, 2048, 256, 512, 512
+FLOPS = 4 * 2 * 512 * 512 * S
+
+F32 = mybir.dt.float32
+BF16 = mybir.dt.bfloat16
+I32 = mybir.dt.int32
+U32 = mybir.dt.uint32
+U16 = mybir.dt.uint16
+U8 = mybir.dt.uint8
+FP8X4 = mybir.dt.float8_e4m3fn_x4
+ALU = mybir.AluOpType
+COPY = mybir.ActivationFunctionType.Copy
+
+P = 128
+PACK = 4
+HALF = 128
+HALVES = S // HALF
+OUT_PIECES = [(0, 128), (128, 128)]
+
+
+def tile_picked_hjoinmedwindtop2_none_po_kernel(
+    tc, x_words, x_scales, w1_words, w1_scales, w2_words, w2_scales, gn, gm, w3_words, w3_scales, w4_words, w4_scales,
+    offs, hz, n1, n2, n3, n4, n5, n6, n7, out_0, out_1, out_2,
+):
+    nc = tc.nc
+    with ExitStack() as ctx:
+        sb = ctx.enter_context(tc.tile_pool(name="sb", bufs=1))
+        ps = ctx.enter_context(tc.psum_pool(name="ps", bufs=1))
+
+        def tile(name, shape, dtype):
+            return sb.tile(shape, dtype, name=name, align_bytes=64)
+
+        def load_list(name, src):
+            t = tile(name, [P, S // 16], U16)
+            nc.sync.dma_start(t[:], src)
+            return t
+
+        def load_words(name, src, width):
+            t = tile(name, [P, width], U32)
+            nc.sync.dma_start(t[:].bitcast(I32), src[0].rearrange("p c r -> p (c r)").bitcast(I32))
+            return t
+
+        def zeroed(name, width):
+            t = tile(name, [P, width], U8)
+            nc.vector.memset(t[:].bitcast(I32), 0)
+            return t
+
+        def load_scale_rows(queues, dst, first, src):
+            for q in range(4):
+                queues[q].dma_start(dst[32 * q + first : 32 * q + first + 4, :].bitcast(I32), src[0, 4 * q : 4 * q + 4, :].bitcast(I32))
+
+        def deal(name, src, dtype, run):
+            t = tile(name, [P, H], dtype)
+            nc.vector.tensor_copy(
+                t[:].rearrange("p (t c i) -> p c t i", t=PACK, i=run),
+                src[:].rearrange("p (c i t) -> p c t i", t=PACK, i=run),
+            )
+            return t
+
+        def entries(lst, start, count):
+            return lst[:, start // 16 : (start + count) // 16]
+
+        def woven(t, run):
+            return t[:].rearrange("p (c i t) -> p c t i", t=PACK, i=run)
+
+        def by_runs(ap, run):
+            return ap.rearrange("p t (c i) -> p c t i", i=run)
+
+        def block(t):
+            return slice(t * P, (t + 1) * P)
+
+        w1s_raw = zeroed("w1s_raw", H)
+        xs = zeroed("xs", T)
+        xs_runs = zeroed("xs_runs", T)
+        w2s_raw = zeroed("w2s_raw", H)
+        w34s_raw = zeroed("w34s_raw", H)
+
+        offs_t = load_list("offs_t", offs)
+        w1w_raw = load_words("w1w_raw", w1_words, H)
+        xw = load_words("xw", x_words, T)
+        load_scale_rows([nc.scalar, nc.scalar, nc.scalar, nc.gpsimd], w1s_raw, 0, w1_scales)
+        load_scale_rows([nc.scalar] * 4, xs, 0, x_scales)
+        load_scale_rows([nc.scalar] * 4, w2s_raw, 0, w2_scales)
+        nc.gpsimd.dma_start(xs_runs[0:P:8, :].bitcast(I32), x_scales[0].bitcast(I32))
+        load_scale_rows([nc.gpsimd] * 4, w34s_raw, 0, w3_scales)
+        load_scale_rows([nc.gpsimd] * 4, w34s_raw, 4, w4_scales)
+        hz_t = load_list("hz_t", hz)
+        n1_t = load_list("n1_t", n1)
+        gn_t = tile("gn_t", [P, PACK], F32)
+        nc.sync.dma_start(gn_t[:], gn.rearrange("(p t) o -> p (t o)", t=PACK))
+        w2w_raw = load_words("w2w_raw", w2_words, H)
+        n2_t = load_list("n2_t", n2)
+        gm_t = tile("gm_t", [P, PACK], F32)
+        nc.sync.dma_start(gm_t[:], gm.rearrange("(p t) o -> p (t o)", t=PACK))
+
+        w1w = deal("w1w", w1w_raw, U32, 4)
+        xq_s = tile("xq_s", [P, S], U8)
+        nc.vector.tensor_copy(xq_s[:], xs[:].indirect(offs_t[:]))
+        w1s = deal("w1s", w1s_raw, U8, 16)
+        w2s = deal("w2s", w2s_raw, U8, 16)
+
+        xq_w = tile("xq_w", [P, S], U32)
+        nc.vector.tensor_copy(xq_w[:], xw[:].indirect(offs_t[:]))
+        hz_bytes = tile("hz_bytes", [P, S], U8)
+        nc.vector.tensor_copy(hz_bytes[:], xs_runs[:].indirect(hz_t[:]))
+        xh_s = tile("xh_s", [P, S], U8)
+        nc.vector.tensor_copy(xh_s[:].bitcast(I32), hz_bytes[:].bitcast(I32))
+        for r in range(1, 4):
+            nc.sync.dma_start(xh_s[r:P:32, :].bitcast(I32), hz_bytes[8 * r : P : 32, :].bitcast(I32))
+        n3_t = load_list("n3_t", n3)
+        n4_t = load_list("n4_t", n4)
+        w3w_raw = load_words("w3w_raw", w3_words, N)
+        w4w_raw = load_words("w4w_raw", w4_words, N)
+        n5_t = load_list("n5_t", n5)
+        n6_t = load_list("n6_t", n6)
+        n7_t = load_list("n7_t", n7)
+
+        xh_w = tile("xh_w", [P, S], U32)
+        nc.vector.tensor_copy(xh_w[:], xw[:].indirect(hz_t[:]))
+        w2w = deal("w2w", w2w_raw, U32, 4)
+
+        y_ps = [ps.tile([P, 2, S], F32, name="y_ps%d" % u, tag="early%d" % u) for u in range(2)]
+        y = [tile("y%d" % t, [P, S], F32) for t in range(PACK)]
+        for t in range(PACK):
+            nc.tensor.matmul_mx(
+                y_ps[t // 2][:, t % 2, :], lhsT=w1w[:, block(t)].bitcast(FP8X4), lhsT_scale=w1s[:, block(t)],
+                rhs=xq_w[:].bitcast(FP8X4), rhs_scale=xq_s[:], start=True, stop=True,
+            )
+        for t in range(PACK):
+            nc.scalar.activation(y[t][:], y_ps[t // 2][:, t % 2, :], COPY, scale=gn_t[:, t : t + 1])
+
+        d_ps = [ps.tile([P, PACK, HALF], F32, name="d_ps%d" % u) for u in range(HALVES)]
+        d = [tile("d%d" % t, [P, S], F32) for t in range(PACK)]
+        for u in range(HALVES):
+            for t in range(PACK):
+                nc.tensor.matmul_mx(
+                    d_ps[u][:, t, :], lhsT=w2w[:, block(t)].bitcast(FP8X4), lhsT_scale=w2s[:, block(t)],
+                    rhs=xh_w[:, block(u)].bitcast(FP8X4), rhs_scale=xh_s[:, block(u)], start=True, stop=True,
+                )
+
+        z_w, z_s = [], []
+        for u in range(HALVES):
+            pa = tile("pa%d" % u, [P, PACK, HALF], BF16)
+            pb = tile("pb%d" % u, [P, PACK, HALF], BF16)
+            for t in range(PACK):
+                nc.scalar.activation(pa[:, t, :], y[t][:].indirect(entries(n1_t, u * HALF, HALF)), COPY)
+                nc.vector.tensor_copy(pb[:, t, :], y[t][:].indirect(entries(n2_t, u * HALF, HALF)))
+            hi = tile("zhi%d" % u, [P, PACK, HALF], BF16)
+            lo = tile("zlo%d" % u, [P, PACK, HALF], BF16)
+            cut = tile("zcut%d" % u, [P, PACK, HALF], BF16)
+            nc.vector.tensor_tensor(hi[:], pa[:], pb[:], ALU.max)
+            nc.vector.tensor_tensor(lo[:], pa[:], pb[:], ALU.min)
+            for t in range(PACK):
+                nc.vector.tensor_tensor(cut[:, t, :], y[t][:, block(u)], hi[:, t, :], ALU.min)
+            z = tile("z%d" % u, [P, PACK * HALF], BF16)
+            nc.vector.tensor_tensor(woven(z, 8), by_runs(lo[:], 8), by_runs(cut[:], 8), ALU.max)
+            z_w.append(tile("z_w%d" % u, [P, HALF], U32))
+            z_s.append(tile("z_s%d" % u, [P, HALF], U8))
+            nc.vector.quantize_mx(z_w[u][:].bitcast(FP8X4), z_s[u][:], z[:])
+
+        for t in range(PACK):
+            for u in range(HALVES):
+                nc.scalar.activation(d[t][:, block(u)], d_ps[u][:, t, :], COPY, scale=gm_t[:, t : t + 1])
+
+        w3w = deal("w3w", w3w_raw, U32, 4)
+        w4w = deal("w4w", w4w_raw, U32, 4)
+        w34s = deal("w34s", w34s_raw, U8, 16)
+
+        h = [tile("h%d" % t, [P, S], F32) for t in range(PACK)]
+        first_ps = [ps.tile([P, 2, HALF], F32, name="h_first%d" % u, tag="early%d" % u) for u in range(2)]
+        last_ps = [ps.tile([P, HALF], F32, name="h_last%d" % t) for t in range(PACK)]
+        for u in range(HALVES):
+            d3 = tile("d3_%d" % u, [P, PACK, HALF], F32)
+            d4 = tile("d4_%d" % u, [P, PACK, HALF], F32)
+            diff = tile("diff%d" % u, [P, PACK, HALF], F32)
+            for t in range(PACK):
+                nc.scalar.activation(d3[:, t, :], d[t][:].indirect(entries(n3_t, u * HALF, HALF)), COPY)
+                nc.scalar.activation(d4[:, t, :], d[t][:].indirect(entries(n4_t, u * HALF, HALF)), COPY)
+                nc.vector.tensor_tensor(diff[:, t, :], d3[:, t, :], d4[:, t, :], ALU.subtract)
+            z2 = tile("z2_%d" % u, [P, PACK * HALF], BF16)
+            nc.vector.tensor_tensor(woven(z2, 4), by_runs(d_ps[u][:], 4), by_runs(diff[:], 4), ALU.mult)
+            z2_w = tile("z2_w%d" % u, [P, HALF], U32)
+            z2_s = tile("z2_s%d" % u, [P, HALF], U8)
+            nc.vector.quantize_mx(z2_w[:].bitcast(FP8X4), z2_s[:], z2[:])
+            for t in range(PACK):
+                acc = first_ps[t // 2][:, t % 2, :] if u == 0 else last_ps[t][:]
+                nc.tensor.matmul_mx(
+                    acc, lhsT=w3w[:, block(t)].bitcast(FP8X4), lhsT_scale=w34s[:, block(t)],
+                    rhs=z_w[u][:].bitcast(FP8X4), rhs_scale=z_s[u][:], start=True, stop=False,
+                )
+                nc.tensor.matmul_mx(
+                    acc, lhsT=w4w[:, block(t)].bitcast(FP8X4), lhsT_scale=w34s[4:P, block(t)],
+                    rhs=z2_w[:].bitcast(FP8X4), rhs_scale=z2_s[:], start=False, stop=True,
+                )
+            for t in range(PACK):
+                acc = first_ps[t // 2][:, t % 2, :] if u == 0 else last_ps[t][:]
+                nc.vector.tensor_copy(h[t][:, block(u)], acc)
+
+        out_w = tile("out_w", [P, S], U32)
+        out_s = tile("out_s", [P, S], U8)
+        out_rows = out_0.rearrange("(p t) j -> p t j", t=PACK)
+        out_words = out_1[0].rearrange("p c r -> p (c r)").bitcast(I32)
+        for v, (start, count) in enumerate(OUT_PIECES):
+            cols = slice(start, start + count)
+            b1, b2, b3, hi, lo, up, top, mid, res = [
+                tile("%s_%d" % (name, v), [P, PACK, count], F32)
+                for name in ("b1", "b2", "b3", "hi", "lo", "up", "top", "mid", "res")
+            ]
+            for t in range(PACK):
+                nc.scalar.activation(b1[:, t, :], h[t][:].indirect(entries(n5_t, start, count)), COPY)
+                nc.scalar.activation(b2[:, t, :], h[t][:].indirect(entries(n6_t, start, count)), COPY)
+                nc.scalar.activation(b3[:, t, :], h[t][:].indirect(entries(n7_t, start, count)), COPY)
+                nc.vector.tensor_tensor(lo[:, t, :], b1[:, t, :], b2[:, t, :], ALU.min)
+                nc.vector.tensor_tensor(hi[:, t, :], b1[:, t, :], b2[:, t, :], ALU.max)
+                nc.vector.tensor_tensor(up[:, t, :], lo[:, t, :], b3[:, t, :], ALU.max)
+                nc.vector.tensor_tensor(top[:, t, :], hi[:, t, :], b3[:, t, :], ALU.max)
+                nc.vector.tensor_tensor(mid[:, t, :], hi[:, t, :], up[:, t, :], ALU.min)
+                nc.vector.scalar_tensor_tensor(res[:, t, :], mid[:, t, :], -0.5, top[:, t, :], ALU.mult, ALU.add)
+            nc.sync.dma_start(out_rows[:, :, cols], res[:])
+            rounded = tile("rounded%d" % v, [P, PACK * count], BF16)
+            nc.vector.tensor_copy(woven(rounded, 4), by_runs(res[:], 4))
+            nc.vector.quantize_mx(out_w[:, cols].bitcast(FP8X4), out_s[:, cols], rounded[:])
+            nc.sync.dma_start(out_words[:, cols], out_w[:, cols].bitcast(I32))
+        for q in range(4):
+            queue = nc.scalar if q < 2 else nc.sync
+            queue.dma_start(out_2[0, 4 * q : 4 * q + 4, :].bitcast(I32), out_s[32 * q : 32 * q + 4, :].bitcast(I32))

@@ -19,7 +19,7 @@ P = 128
 PACK = 4
 HALF = 128
 HALVES = S // HALF
-OUT_PIECES = [(0, 128), (128, 128)]
+N2_ON_VECTOR = 3
 
 
 def tile_picked_hjoinmedwindtop2_none_po_kernel(
@@ -31,30 +31,30 @@ def tile_picked_hjoinmedwindtop2_none_po_kernel(
         sb = ctx.enter_context(tc.tile_pool(name="sb", bufs=1))
         ps = ctx.enter_context(tc.psum_pool(name="ps", bufs=1))
 
-        def tile(name, shape, dtype):
-            return sb.tile(shape, dtype, name=name, align_bytes=64)
+        def tile(name, shape, dtype, tag=None):
+            return sb.tile(shape, dtype, name=name, tag=tag or name, align_bytes=64)
 
         def load_list(name, src):
             t = tile(name, [P, S // 16], U16)
             nc.sync.dma_start(t[:], src)
             return t
 
-        def load_words(name, src, width):
-            t = tile(name, [P, width], U32)
+        def load_words(name, src, width, tag=None):
+            t = tile(name, [P, width], U32, tag)
             nc.sync.dma_start(t[:].bitcast(I32), src[0].rearrange("p c r -> p (c r)").bitcast(I32))
             return t
 
-        def zeroed(name, width):
-            t = tile(name, [P, width], U8)
+        def zeroed(name, width, tag=None):
+            t = tile(name, [P, width], U8, tag)
             nc.vector.memset(t[:].bitcast(I32), 0)
             return t
 
-        def load_scale_rows(queues, dst, first, src):
+        def load_scale_rows(queue, dst, first, src):
             for q in range(4):
-                queues[q].dma_start(dst[32 * q + first : 32 * q + first + 4, :].bitcast(I32), src[0, 4 * q : 4 * q + 4, :].bitcast(I32))
+                queue.dma_start(dst[32 * q + first : 32 * q + first + 4, :].bitcast(I32), src[0, 4 * q : 4 * q + 4, :].bitcast(I32))
 
-        def deal(name, src, dtype, run):
-            t = tile(name, [P, H], dtype)
+        def deal(name, src, dtype, run, tag):
+            t = tile(name, [P, H], dtype, tag)
             nc.vector.tensor_copy(
                 t[:].rearrange("p (t c i) -> p c t i", t=PACK, i=run),
                 src[:].rearrange("p (c i t) -> p c t i", t=PACK, i=run),
@@ -73,68 +73,74 @@ def tile_picked_hjoinmedwindtop2_none_po_kernel(
         def block(t):
             return slice(t * P, (t + 1) * P)
 
-        w1s_raw = zeroed("w1s_raw", H)
+        def load_gain(name, src):
+            t = tile(name, [P, PACK], F32)
+            nc.gpsimd.dma_start(t[:], src.rearrange("(p t) o -> p (t o)", t=PACK))
+            return t
+
         xs = zeroed("xs", T)
         xs_runs = zeroed("xs_runs", T)
+        w1s_raw = zeroed("w1s_raw", H)
         w2s_raw = zeroed("w2s_raw", H)
-        w34s_raw = zeroed("w34s_raw", H)
+        zeros = tile("zeros", [P, S], F32)
+        nc.vector.memset(zeros[:], 0.0)
+        y = [tile("y%d" % t, [P, 2 * S], F32) for t in range(PACK)]
+        d = [tile("d%d" % t, [P, 2 * S], F32) for t in range(PACK)]
+        for window in y + d:
+            nc.scalar.activation(window[:, S:], zeros[:], COPY)
 
         offs_t = load_list("offs_t", offs)
         w1w_raw = load_words("w1w_raw", w1_words, H)
-        xw = load_words("xw", x_words, T)
-        load_scale_rows([nc.scalar, nc.scalar, nc.scalar, nc.gpsimd], w1s_raw, 0, w1_scales)
-        load_scale_rows([nc.scalar] * 4, xs, 0, x_scales)
-        load_scale_rows([nc.scalar] * 4, w2s_raw, 0, w2_scales)
-        nc.gpsimd.dma_start(xs_runs[0:P:8, :].bitcast(I32), x_scales[0].bitcast(I32))
-        load_scale_rows([nc.gpsimd] * 4, w34s_raw, 0, w3_scales)
-        load_scale_rows([nc.gpsimd] * 4, w34s_raw, 4, w4_scales)
+        load_scale_rows(nc.sync, xs, 0, x_scales)
         hz_t = load_list("hz_t", hz)
+        xw = load_words("xw", x_words, T)
+        load_scale_rows(nc.sync, w1s_raw, 0, w1_scales)
+        nc.sync.dma_start(xs_runs[0:P:8, :].bitcast(I32), x_scales[0].bitcast(I32))
         n1_t = load_list("n1_t", n1)
-        gn_t = tile("gn_t", [P, PACK], F32)
-        nc.sync.dma_start(gn_t[:], gn.rearrange("(p t) o -> p (t o)", t=PACK))
-        w2w_raw = load_words("w2w_raw", w2_words, H)
+        gn_t = load_gain("gn_t", gn)
         n2_t = load_list("n2_t", n2)
-        gm_t = tile("gm_t", [P, PACK], F32)
-        nc.sync.dma_start(gm_t[:], gm.rearrange("(p t) o -> p (t o)", t=PACK))
-
-        w1w = deal("w1w", w1w_raw, U32, 4)
-        xq_s = tile("xq_s", [P, S], U8)
-        nc.vector.tensor_copy(xq_s[:], xs[:].indirect(offs_t[:]))
-        w1s = deal("w1s", w1s_raw, U8, 16)
-        w2s = deal("w2s", w2s_raw, U8, 16)
-
-        xq_w = tile("xq_w", [P, S], U32)
-        nc.vector.tensor_copy(xq_w[:], xw[:].indirect(offs_t[:]))
-        hz_bytes = tile("hz_bytes", [P, S], U8)
-        nc.vector.tensor_copy(hz_bytes[:], xs_runs[:].indirect(hz_t[:]))
-        xh_s = tile("xh_s", [P, S], U8)
-        nc.vector.tensor_copy(xh_s[:].bitcast(I32), hz_bytes[:].bitcast(I32))
-        for r in range(1, 4):
-            nc.sync.dma_start(xh_s[r:P:32, :].bitcast(I32), hz_bytes[8 * r : P : 32, :].bitcast(I32))
+        w2w_raw = load_words("w2w_raw", w2_words, H)
+        load_scale_rows(nc.gpsimd, w2s_raw, 0, w2_scales)
+        gm_t = load_gain("gm_t", gm)
         n3_t = load_list("n3_t", n3)
         n4_t = load_list("n4_t", n4)
-        w3w_raw = load_words("w3w_raw", w3_words, N)
-        w4w_raw = load_words("w4w_raw", w4_words, N)
         n5_t = load_list("n5_t", n5)
         n6_t = load_list("n6_t", n6)
         n7_t = load_list("n7_t", n7)
 
+        w1w = deal("w1w", w1w_raw, U32, 4, "w_words")
+        xq_s = tile("xq_s", [P, S], U8)
+        nc.vector.tensor_copy(xq_s[:], xs[:].indirect(offs_t[:]))
+        xq_w = tile("xq_w", [P, S], U32, "picked")
+        nc.vector.tensor_copy(xq_w[:], xw[:].indirect(offs_t[:]))
+        w1s = deal("w1s", w1s_raw, U8, 16, "w_scales")
         xh_w = tile("xh_w", [P, S], U32)
         nc.vector.tensor_copy(xh_w[:], xw[:].indirect(hz_t[:]))
-        w2w = deal("w2w", w2w_raw, U32, 4)
 
         y_ps = [ps.tile([P, 2, S], F32, name="y_ps%d" % u, tag="early%d" % u) for u in range(2)]
-        y = [tile("y%d" % t, [P, S], F32) for t in range(PACK)]
         for t in range(PACK):
             nc.tensor.matmul_mx(
                 y_ps[t // 2][:, t % 2, :], lhsT=w1w[:, block(t)].bitcast(FP8X4), lhsT_scale=w1s[:, block(t)],
                 rhs=xq_w[:].bitcast(FP8X4), rhs_scale=xq_s[:], start=True, stop=True,
             )
+        hz_bytes = tile("hz_bytes", [P, S], U8, "picked")
+        nc.vector.tensor_copy(hz_bytes[:], xs_runs[:].indirect(hz_t[:]))
+        xh_s = tile("xh_s", [P, S], U8)
+        nc.vector.tensor_copy(xh_s[:].bitcast(I32), hz_bytes[:].bitcast(I32))
+        for r in range(1, 4):
+            nc.sync.dma_start(xh_s[r:P:32, :].bitcast(I32), hz_bytes[8 * r : P : 32, :].bitcast(I32))
+        w2w = deal("w2w", w2w_raw, U32, 4, "w_words")
+        w2s = deal("w2s", w2s_raw, U8, 16, "w_scales")
+        w4w_raw = load_words("w4w_raw", w4_words, N, "w2w_raw")
+        w3w_raw = load_words("w3w_raw", w3_words, N, "picked")
+        w34s_raw = zeroed("w34s_raw", H, "xs_runs")
+        load_scale_rows(nc.sync, w34s_raw, 0, w3_scales)
+        load_scale_rows(nc.sync, w34s_raw, 4, w4_scales)
+
         for t in range(PACK):
-            nc.scalar.activation(y[t][:], y_ps[t // 2][:, t % 2, :], COPY, scale=gn_t[:, t : t + 1])
+            nc.scalar.activation(y[t][:, :S], y_ps[t // 2][:, t % 2, :], COPY, scale=gn_t[:, t : t + 1])
 
         d_ps = [ps.tile([P, PACK, HALF], F32, name="d_ps%d" % u) for u in range(HALVES)]
-        d = [tile("d%d" % t, [P, S], F32) for t in range(PACK)]
         for u in range(HALVES):
             for t in range(PACK):
                 nc.tensor.matmul_mx(
@@ -142,45 +148,50 @@ def tile_picked_hjoinmedwindtop2_none_po_kernel(
                     rhs=xh_w[:, block(u)].bitcast(FP8X4), rhs_scale=xh_s[:, block(u)], start=True, stop=True,
                 )
 
-        z_w, z_s = [], []
-        for u in range(HALVES):
-            pa = tile("pa%d" % u, [P, PACK, HALF], BF16)
-            pb = tile("pb%d" % u, [P, PACK, HALF], BF16)
-            for t in range(PACK):
-                nc.scalar.activation(pa[:, t, :], y[t][:].indirect(entries(n1_t, u * HALF, HALF)), COPY)
-                nc.vector.tensor_copy(pb[:, t, :], y[t][:].indirect(entries(n2_t, u * HALF, HALF)))
-            hi = tile("zhi%d" % u, [P, PACK, HALF], BF16)
-            lo = tile("zlo%d" % u, [P, PACK, HALF], BF16)
-            cut = tile("zcut%d" % u, [P, PACK, HALF], BF16)
-            nc.vector.tensor_tensor(hi[:], pa[:], pb[:], ALU.max)
-            nc.vector.tensor_tensor(lo[:], pa[:], pb[:], ALU.min)
-            for t in range(PACK):
-                nc.vector.tensor_tensor(cut[:, t, :], y[t][:, block(u)], hi[:, t, :], ALU.min)
-            z = tile("z%d" % u, [P, PACK * HALF], BF16)
-            nc.vector.tensor_tensor(woven(z, 8), by_runs(lo[:], 8), by_runs(cut[:], 8), ALU.max)
-            z_w.append(tile("z_w%d" % u, [P, HALF], U32))
-            z_s.append(tile("z_s%d" % u, [P, HALF], U8))
-            nc.vector.quantize_mx(z_w[u][:].bitcast(FP8X4), z_s[u][:], z[:])
-
+        pa, pb, zhi, zlo, cut = [tile(name, [P, PACK, S], BF16) for name in ("pa", "pb", "zhi", "zlo", "cut")]
         for t in range(PACK):
-            for u in range(HALVES):
+            nc.scalar.activation(pa[:, t, :], y[t][:].indirect(n1_t[:]), COPY)
+            if t < N2_ON_VECTOR:
+                nc.vector.tensor_copy(pb[:, t, :], y[t][:].indirect(n2_t[:]))
+            else:
+                nc.scalar.activation(pb[:, t, :], y[t][:].indirect(n2_t[:]), COPY)
+            if t % 2 == 1:
+                g = slice(t - 1, t + 1)
+                nc.vector.tensor_tensor(zhi[:, g, :], pa[:, g, :], pb[:, g, :], ALU.max)
+                nc.vector.tensor_tensor(zlo[:, g, :], pa[:, g, :], pb[:, g, :], ALU.min)
+                for r in (t - 1, t):
+                    nc.vector.tensor_tensor(cut[:, r, :], y[r][:, :S], zhi[:, r, :], ALU.min)
+        z = tile("z", [P, PACK * S], BF16)
+        nc.vector.tensor_tensor(woven(z, 8), by_runs(zlo[:], 8), by_runs(cut[:], 8), ALU.max)
+        z_w = tile("z_w", [P, S], U32)
+        z_s = tile("z_s", [P, S], U8)
+        nc.vector.quantize_mx(z_w[:].bitcast(FP8X4), z_s[:], z[:])
+
+        for u in range(HALVES):
+            for t in range(PACK):
                 nc.scalar.activation(d[t][:, block(u)], d_ps[u][:, t, :], COPY, scale=gm_t[:, t : t + 1])
 
-        w3w = deal("w3w", w3w_raw, U32, 4)
-        w4w = deal("w4w", w4w_raw, U32, 4)
-        w34s = deal("w34s", w34s_raw, U8, 16)
+        w3w = deal("w3w", w3w_raw, U32, 4, "cut")
+        w4w = deal("w4w", w4w_raw, U32, 4, "zlo")
+        w34s = deal("w34s", w34s_raw, U8, 16, "z")
 
-        h = [tile("h%d" % t, [P, S], F32) for t in range(PACK)]
+        h = y
         first_ps = [ps.tile([P, 2, HALF], F32, name="h_first%d" % u, tag="early%d" % u) for u in range(2)]
         last_ps = [ps.tile([P, HALF], F32, name="h_last%d" % t) for t in range(PACK)]
+        d3, d4 = [tile(name, [P, PACK, S], F32) for name in ("at_n3", "at_n4")]
+
+        def fetch_d(tiles, start, count):
+            cols = slice(start, start + count)
+            for t in tiles:
+                nc.scalar.activation(d3[:, t, cols], d[t][:].indirect(entries(n3_t, start, count)), COPY)
+                nc.scalar.activation(d4[:, t, cols], d[t][:].indirect(entries(n4_t, start, count)), COPY)
+
+        fetch_d([0, 1], 0, S)
         for u in range(HALVES):
-            d3 = tile("d3_%d" % u, [P, PACK, HALF], F32)
-            d4 = tile("d4_%d" % u, [P, PACK, HALF], F32)
-            diff = tile("diff%d" % u, [P, PACK, HALF], F32)
-            for t in range(PACK):
-                nc.scalar.activation(d3[:, t, :], d[t][:].indirect(entries(n3_t, u * HALF, HALF)), COPY)
-                nc.scalar.activation(d4[:, t, :], d[t][:].indirect(entries(n4_t, u * HALF, HALF)), COPY)
-                nc.vector.tensor_tensor(diff[:, t, :], d3[:, t, :], d4[:, t, :], ALU.subtract)
+            fetch_d([2, 3], u * HALF, HALF)
+            diff = tile("diff%d" % u, [P, PACK, HALF], F32, "diff0" if u == 0 else "z2_0")
+            for g in [slice(0, 2), slice(2, 4)] if u == 0 else [slice(0, 4)]:
+                nc.vector.tensor_tensor(diff[:, g, :], d3[:, g, block(u)], d4[:, g, block(u)], ALU.subtract)
             z2 = tile("z2_%d" % u, [P, PACK * HALF], BF16)
             nc.vector.tensor_tensor(woven(z2, 4), by_runs(d_ps[u][:], 4), by_runs(diff[:], 4), ALU.mult)
             z2_w = tile("z2_w%d" % u, [P, HALF], U32)
@@ -190,7 +201,7 @@ def tile_picked_hjoinmedwindtop2_none_po_kernel(
                 acc = first_ps[t // 2][:, t % 2, :] if u == 0 else last_ps[t][:]
                 nc.tensor.matmul_mx(
                     acc, lhsT=w3w[:, block(t)].bitcast(FP8X4), lhsT_scale=w34s[:, block(t)],
-                    rhs=z_w[u][:].bitcast(FP8X4), rhs_scale=z_s[u][:], start=True, stop=False,
+                    rhs=z_w[:, block(u)].bitcast(FP8X4), rhs_scale=z_s[:, block(u)], start=True, stop=False,
                 )
                 nc.tensor.matmul_mx(
                     acc, lhsT=w4w[:, block(t)].bitcast(FP8X4), lhsT_scale=w34s[4:P, block(t)],
@@ -198,31 +209,41 @@ def tile_picked_hjoinmedwindtop2_none_po_kernel(
                 )
             for t in range(PACK):
                 acc = first_ps[t // 2][:, t % 2, :] if u == 0 else last_ps[t][:]
-                nc.vector.tensor_copy(h[t][:, block(u)], acc)
+                if u == 0:
+                    nc.scalar.copy(h[t][:, block(u)], acc)
+                else:
+                    nc.vector.tensor_copy(h[t][:, block(u)], acc)
 
         out_w = tile("out_w", [P, S], U32)
         out_s = tile("out_s", [P, S], U8)
         out_rows = out_0.rearrange("(p t) j -> p t j", t=PACK)
         out_words = out_1[0].rearrange("p c r -> p (c r)").bitcast(I32)
-        for v, (start, count) in enumerate(OUT_PIECES):
+        b1, b2, b3, hi, lo, up, top, mid, res = [
+            tile(name, [P, PACK, S], F32) for name in ("b1", "b2", "b3", "hi", "lo", "up", "top", "mid", "res")
+        ]
+
+        def combine(tiles, start, count):
             cols = slice(start, start + count)
-            b1, b2, b3, hi, lo, up, top, mid, res = [
-                tile("%s_%d" % (name, v), [P, PACK, count], F32)
-                for name in ("b1", "b2", "b3", "hi", "lo", "up", "top", "mid", "res")
-            ]
-            for t in range(PACK):
-                nc.scalar.activation(b1[:, t, :], h[t][:].indirect(entries(n5_t, start, count)), COPY)
-                nc.scalar.activation(b2[:, t, :], h[t][:].indirect(entries(n6_t, start, count)), COPY)
-                nc.scalar.activation(b3[:, t, :], h[t][:].indirect(entries(n7_t, start, count)), COPY)
-                nc.vector.tensor_tensor(lo[:, t, :], b1[:, t, :], b2[:, t, :], ALU.min)
-                nc.vector.tensor_tensor(hi[:, t, :], b1[:, t, :], b2[:, t, :], ALU.max)
-                nc.vector.tensor_tensor(up[:, t, :], lo[:, t, :], b3[:, t, :], ALU.max)
-                nc.vector.tensor_tensor(top[:, t, :], hi[:, t, :], b3[:, t, :], ALU.max)
-                nc.vector.tensor_tensor(mid[:, t, :], hi[:, t, :], up[:, t, :], ALU.min)
-                nc.vector.scalar_tensor_tensor(res[:, t, :], mid[:, t, :], -0.5, top[:, t, :], ALU.mult, ALU.add)
-            nc.sync.dma_start(out_rows[:, :, cols], res[:])
-            rounded = tile("rounded%d" % v, [P, PACK * count], BF16)
-            nc.vector.tensor_copy(woven(rounded, 4), by_runs(res[:], 4))
+            for b, lst in ((b1, n5_t), (b2, n6_t), (b3, n7_t)):
+                for t in tiles:
+                    nc.scalar.activation(b[:, t, cols], h[t][:].indirect(entries(lst, start, count)), COPY)
+            g = slice(tiles[0], tiles[-1] + 1)
+            nc.vector.tensor_tensor(lo[:, g, cols], b1[:, g, cols], b2[:, g, cols], ALU.min)
+            nc.vector.tensor_tensor(hi[:, g, cols], b1[:, g, cols], b2[:, g, cols], ALU.max)
+            nc.vector.tensor_tensor(up[:, g, cols], lo[:, g, cols], b3[:, g, cols], ALU.max)
+            nc.vector.tensor_tensor(top[:, g, cols], hi[:, g, cols], b3[:, g, cols], ALU.max)
+            nc.vector.tensor_tensor(mid[:, g, cols], hi[:, g, cols], up[:, g, cols], ALU.min)
+            nc.vector.scalar_tensor_tensor(res[:, g, cols], mid[:, g, cols], -0.5, top[:, g, cols], ALU.mult, ALU.add)
+
+        combine([0], 0, S)
+        combine([1], 0, S)
+        nc.sync.dma_start(out_rows[:, 0:2, :], res[:, 0:2, :])
+        for u in range(HALVES):
+            cols = block(u)
+            combine([2, 3], u * HALF, HALF)
+            nc.sync.dma_start(out_rows[:, 2:4, cols], res[:, 2:4, cols])
+            rounded = tile("rounded%d" % u, [P, PACK * HALF], BF16)
+            nc.scalar.copy(woven(rounded, 4), by_runs(res[:, :, cols], 4))
             nc.vector.quantize_mx(out_w[:, cols].bitcast(FP8X4), out_s[:, cols], rounded[:])
             nc.sync.dma_start(out_words[:, cols], out_w[:, cols].bitcast(I32))
         for q in range(4):

@@ -19,7 +19,7 @@ P = 128
 PACK = 4
 HALF = 128
 HALVES = S // HALF
-N2_ON_VECTOR = 3
+N2_ON_VECTOR = 4
 
 
 def tile_picked_hjoinmedwindtop2_none_po_kernel(
@@ -44,9 +44,9 @@ def tile_picked_hjoinmedwindtop2_none_po_kernel(
             nc.sync.dma_start(t[:].bitcast(I32), src[0].rearrange("p c r -> p (c r)").bitcast(I32))
             return t
 
-        def zeroed(name, width, tag=None):
+        def zeroed(engine, name, width, tag=None):
             t = tile(name, [P, width], U8, tag)
-            nc.vector.memset(t[:].bitcast(I32), 0)
+            engine.memset(t[:].bitcast(I32), 0)
             return t
 
         def load_scale_rows(queue, dst, first, src):
@@ -78,10 +78,10 @@ def tile_picked_hjoinmedwindtop2_none_po_kernel(
             nc.gpsimd.dma_start(t[:], src.rearrange("(p t) o -> p (t o)", t=PACK))
             return t
 
-        xs = zeroed("xs", T)
-        xs_runs = zeroed("xs_runs", T)
-        w1s_raw = zeroed("w1s_raw", H)
-        w2s_raw = zeroed("w2s_raw", H)
+        xs = zeroed(nc.gpsimd, "xs", T)
+        xs_runs = zeroed(nc.vector, "xs_runs", T)
+        w1s_raw = zeroed(nc.vector, "w1s_raw", H)
+        w2s_raw = zeroed(nc.vector, "w2s_raw", H)
         zeros = tile("zeros", [P, S], F32)
         nc.vector.memset(zeros[:], 0.0)
         y = [tile("y%d" % t, [P, 2 * S], F32) for t in range(PACK)]
@@ -111,19 +111,19 @@ def tile_picked_hjoinmedwindtop2_none_po_kernel(
         w1w = deal("w1w", w1w_raw, U32, 4, "w_words")
         xq_s = tile("xq_s", [P, S], U8)
         nc.vector.tensor_copy(xq_s[:], xs[:].indirect(offs_t[:]))
-        xq_w = tile("xq_w", [P, S], U32, "picked")
+        xq_w = tile("xq_w", [P, S], U32)
         nc.vector.tensor_copy(xq_w[:], xw[:].indirect(offs_t[:]))
         w1s = deal("w1s", w1s_raw, U8, 16, "w_scales")
         xh_w = tile("xh_w", [P, S], U32)
         nc.vector.tensor_copy(xh_w[:], xw[:].indirect(hz_t[:]))
 
-        y_ps = [ps.tile([P, 2, S], F32, name="y_ps%d" % u, tag="early%d" % u) for u in range(2)]
+        y_ps = [ps.tile([P, S], F32, name="y_ps%d" % t, tag="bank%d" % t) for t in range(PACK)]
         for t in range(PACK):
             nc.tensor.matmul_mx(
-                y_ps[t // 2][:, t % 2, :], lhsT=w1w[:, block(t)].bitcast(FP8X4), lhsT_scale=w1s[:, block(t)],
+                y_ps[t][:], lhsT=w1w[:, block(t)].bitcast(FP8X4), lhsT_scale=w1s[:, block(t)],
                 rhs=xq_w[:].bitcast(FP8X4), rhs_scale=xq_s[:], start=True, stop=True,
             )
-        hz_bytes = tile("hz_bytes", [P, S], U8, "picked")
+        hz_bytes = tile("hz_bytes", [P, S], U8, "xw")
         nc.vector.tensor_copy(hz_bytes[:], xs_runs[:].indirect(hz_t[:]))
         xh_s = tile("xh_s", [P, S], U8)
         nc.vector.tensor_copy(xh_s[:].bitcast(I32), hz_bytes[:].bitcast(I32))
@@ -132,13 +132,13 @@ def tile_picked_hjoinmedwindtop2_none_po_kernel(
         w2w = deal("w2w", w2w_raw, U32, 4, "w_words")
         w2s = deal("w2s", w2s_raw, U8, 16, "w_scales")
         w4w_raw = load_words("w4w_raw", w4_words, N, "w2w_raw")
-        w3w_raw = load_words("w3w_raw", w3_words, N, "picked")
-        w34s_raw = zeroed("w34s_raw", H, "xs_runs")
+        w3w_raw = load_words("w3w_raw", w3_words, N, "w2s_raw")
+        w34s_raw = zeroed(nc.vector, "w34s_raw", H, "xs_runs")
         load_scale_rows(nc.sync, w34s_raw, 0, w3_scales)
         load_scale_rows(nc.sync, w34s_raw, 4, w4_scales)
 
         for t in range(PACK):
-            nc.scalar.activation(y[t][:, :S], y_ps[t // 2][:, t % 2, :], COPY, scale=gn_t[:, t : t + 1])
+            nc.scalar.activation(y[t][:, :S], y_ps[t][:], COPY, scale=gn_t[:, t : t + 1])
 
         d_ps = [ps.tile([P, PACK, HALF], F32, name="d_ps%d" % u) for u in range(HALVES)]
         for u in range(HALVES):
@@ -176,8 +176,8 @@ def tile_picked_hjoinmedwindtop2_none_po_kernel(
         w34s = deal("w34s", w34s_raw, U8, 16, "z")
 
         h = y
-        first_ps = [ps.tile([P, 2, HALF], F32, name="h_first%d" % u, tag="early%d" % u) for u in range(2)]
-        last_ps = [ps.tile([P, HALF], F32, name="h_last%d" % t) for t in range(PACK)]
+        first_ps = [ps.tile([P, 2, HALF], F32, name="h_first%d" % u) for u in range(2)]
+        last_ps = [ps.tile([P, HALF], F32, name="h_last%d" % t, tag="bank%d" % t) for t in range(PACK)]
         d3, d4 = [tile(name, [P, PACK, S], F32) for name in ("at_n3", "at_n4")]
 
         def fetch_d(tiles, start, count):
@@ -189,12 +189,12 @@ def tile_picked_hjoinmedwindtop2_none_po_kernel(
         fetch_d([0, 1], 0, S)
         for u in range(HALVES):
             fetch_d([2, 3], u * HALF, HALF)
-            diff = tile("diff%d" % u, [P, PACK, HALF], F32, "diff0" if u == 0 else "z2_0")
+            diff = tile("diff%d" % u, [P, PACK, HALF], F32, "xs_runs" if u == 0 else "w2s_raw")
             for g in [slice(0, 2), slice(2, 4)] if u == 0 else [slice(0, 4)]:
                 nc.vector.tensor_tensor(diff[:, g, :], d3[:, g, block(u)], d4[:, g, block(u)], ALU.subtract)
-            z2 = tile("z2_%d" % u, [P, PACK * HALF], BF16)
+            z2 = tile("z2_%d" % u, [P, PACK * HALF], BF16, "w2s_raw" if u == 0 else None)
             nc.vector.tensor_tensor(woven(z2, 4), by_runs(d_ps[u][:], 4), by_runs(diff[:], 4), ALU.mult)
-            z2_w = tile("z2_w%d" % u, [P, HALF], U32)
+            z2_w = tile("z2_w%d" % u, [P, HALF], U32, "w2w_raw" if u == 0 else None)
             z2_s = tile("z2_s%d" % u, [P, HALF], U8)
             nc.vector.quantize_mx(z2_w[:].bitcast(FP8X4), z2_s[:], z2[:])
             for t in range(PACK):
@@ -240,10 +240,14 @@ def tile_picked_hjoinmedwindtop2_none_po_kernel(
         nc.sync.dma_start(out_rows[:, 0:2, :], res[:, 0:2, :])
         for u in range(HALVES):
             cols = block(u)
-            combine([2, 3], u * HALF, HALF)
+            for tiles in [[2, 3]] if u == 0 else [[2], [3]]:
+                combine(tiles, u * HALF, HALF)
             nc.sync.dma_start(out_rows[:, 2:4, cols], res[:, 2:4, cols])
             rounded = tile("rounded%d" % u, [P, PACK * HALF], BF16)
-            nc.scalar.copy(woven(rounded, 4), by_runs(res[:, :, cols], 4))
+            if u == 0:
+                nc.scalar.copy(woven(rounded, 4), by_runs(res[:, :, cols], 4))
+            else:
+                nc.vector.tensor_copy(woven(rounded, 4), by_runs(res[:, :, cols], 4))
             nc.vector.quantize_mx(out_w[:, cols].bitcast(FP8X4), out_s[:, cols], rounded[:])
             nc.sync.dma_start(out_words[:, cols], out_w[:, cols].bitcast(I32))
         for q in range(4):

@@ -44,13 +44,13 @@ def tile_picked_hjoinmedwindtop2_none_po_kernel(
             nc.sync.dma_start(t[:].bitcast(I32), src[0].rearrange("p c r -> p (c r)").bitcast(I32))
             return t
 
-        def zeroed(engine, name, width, tag=None):
-            t = tile(name, [P, width], U8, tag)
-            engine.memset(t[:].bitcast(I32), 0)
+        def zeroed(name, width):
+            t = tile(name, [P, width], U8)
+            nc.vector.memset(t[:].bitcast(I32), 0)
             return t
 
-        def load_scale_rows(queue, dst, first, src):
-            for q in range(4):
+        def load_scale_rows(queues, dst, first, src):
+            for q, queue in enumerate(queues):
                 queue.dma_start(dst[32 * q + first : 32 * q + first + 4, :].bitcast(I32), src[0, 4 * q : 4 * q + 4, :].bitcast(I32))
 
         def deal(name, src, dtype, run, tag):
@@ -75,38 +75,43 @@ def tile_picked_hjoinmedwindtop2_none_po_kernel(
 
         def load_gain(name, src):
             t = tile(name, [P, PACK], F32)
-            nc.gpsimd.dma_start(t[:], src.rearrange("(p t) o -> p (t o)", t=PACK))
+            nc.sync.dma_start(t[:], src.rearrange("(p t) o -> p (t o)", t=PACK))
             return t
 
-        xs = zeroed(nc.gpsimd, "xs", T)
-        xs_runs = zeroed(nc.vector, "xs_runs", T)
-        w1s_raw = zeroed(nc.vector, "w1s_raw", H)
-        w2s_raw = zeroed(nc.vector, "w2s_raw", H)
-        zeros = tile("zeros", [P, S], F32)
-        nc.vector.memset(zeros[:], 0.0)
-        y = [tile("y%d" % t, [P, 2 * S], F32) for t in range(PACK)]
-        d = [tile("d%d" % t, [P, 2 * S], F32) for t in range(PACK)]
-        for window in y + d:
-            nc.scalar.activation(window[:, S:], zeros[:], COPY)
+        w1s_raw = zeroed("w1s_raw", H)
+        xs = zeroed("xs", T)
+        xs_runs = zeroed("xs_runs", T)
+        w2s_raw = zeroed("w2s_raw", H)
+        w34s_raw = zeroed("w34s_raw", H)
 
         offs_t = load_list("offs_t", offs)
-        w1w_raw = load_words("w1w_raw", w1_words, H)
-        load_scale_rows(nc.sync, xs, 0, x_scales)
         hz_t = load_list("hz_t", hz)
+        w1w_raw = load_words("w1w_raw", w1_words, H)
         xw = load_words("xw", x_words, T)
-        load_scale_rows(nc.sync, w1s_raw, 0, w1_scales)
-        nc.sync.dma_start(xs_runs[0:P:8, :].bitcast(I32), x_scales[0].bitcast(I32))
+        load_scale_rows([nc.scalar, nc.scalar, nc.scalar, nc.gpsimd], w1s_raw, 0, w1_scales)
+        load_scale_rows([nc.scalar] * 4, xs, 0, x_scales)
+        nc.gpsimd.dma_start(xs_runs[0:P:8, :].bitcast(I32), x_scales[0].bitcast(I32))
+        load_scale_rows([nc.gpsimd] * 4, w2s_raw, 0, w2_scales)
+        load_scale_rows([nc.gpsimd] * 4, w34s_raw, 0, w3_scales)
         n1_t = load_list("n1_t", n1)
         gn_t = load_gain("gn_t", gn)
         n2_t = load_list("n2_t", n2)
         w2w_raw = load_words("w2w_raw", w2_words, H)
-        load_scale_rows(nc.gpsimd, w2s_raw, 0, w2_scales)
         gm_t = load_gain("gm_t", gm)
         n3_t = load_list("n3_t", n3)
         n4_t = load_list("n4_t", n4)
         n5_t = load_list("n5_t", n5)
         n6_t = load_list("n6_t", n6)
         n7_t = load_list("n7_t", n7)
+        load_scale_rows([nc.sync] * 4, w34s_raw, 4, w4_scales)
+
+        zeros = tile("zeros", [P, S], F32)
+        nc.vector.memset(zeros[:], 0.0)
+        y = [tile("y%d" % t, [P, 2 * S], F32) for t in range(PACK)]
+        d = [tile("d%d" % t, [P, 2 * S], F32) for t in range(PACK)]
+        for t in range(PACK):
+            nc.scalar.activation(y[t][:, S:], zeros[:], COPY)
+            nc.vector.memset(d[t][:, S:], 0.0)
 
         w1w = deal("w1w", w1w_raw, U32, 4, "w_words")
         xq_s = tile("xq_s", [P, S], U8)
@@ -133,9 +138,6 @@ def tile_picked_hjoinmedwindtop2_none_po_kernel(
         w2s = deal("w2s", w2s_raw, U8, 16, "w_scales")
         w4w_raw = load_words("w4w_raw", w4_words, N, "w2w_raw")
         w3w_raw = load_words("w3w_raw", w3_words, N, "w2s_raw")
-        w34s_raw = zeroed(nc.vector, "w34s_raw", H, "xs_runs")
-        load_scale_rows(nc.sync, w34s_raw, 0, w3_scales)
-        load_scale_rows(nc.sync, w34s_raw, 4, w4_scales)
 
         for t in range(PACK):
             nc.scalar.activation(y[t][:, :S], y_ps[t][:], COPY, scale=gn_t[:, t : t + 1])
@@ -189,7 +191,7 @@ def tile_picked_hjoinmedwindtop2_none_po_kernel(
         fetch_d([0, 1], 0, S)
         for u in range(HALVES):
             fetch_d([2, 3], u * HALF, HALF)
-            diff = tile("diff%d" % u, [P, PACK, HALF], F32, "xs_runs" if u == 0 else "w2s_raw")
+            diff = tile("diff%d" % u, [P, PACK, HALF], F32, "w34s_raw" if u == 0 else "w2s_raw")
             for g in [slice(0, 2), slice(2, 4)] if u == 0 else [slice(0, 4)]:
                 nc.vector.tensor_tensor(diff[:, g, :], d3[:, g, block(u)], d4[:, g, block(u)], ALU.subtract)
             z2 = tile("z2_%d" % u, [P, PACK * HALF], BF16, "w2s_raw" if u == 0 else None)

from contextlib import ExitStack

import concourse.mybir as mybir

K, T, S, N, H = 512, 2048, 256, 512, 512
FLOPS = 4 * 2 * 512 * 512 * S

F32 = mybir.dt.float32
BF16 = mybir.dt.bfloat16
I32 = mybir.dt.int32
U32 = mybir.dt.uint32
U16 = mybir.dt.uint16
U8 = mybir.dt.uint8
FP8X4 = mybir.dt.float8_e4m3fn_x4
ALU = mybir.AluOpType
COPY = mybir.ActivationFunctionType.Copy

P = 128
PACK = 4
HALF = 128
HALVES = S // HALF
N2_ON_VECTOR = 4


def tile_picked_hjoinmedwindtop2_none_po_kernel(
    tc, x_words, x_scales, w1_words, w1_scales, w2_words, w2_scales, gn, gm, w3_words, w3_scales, w4_words, w4_scales,
    offs, hz, n1, n2, n3, n4, n5, n6, n7, out_0, out_1, out_2,
):
    nc = tc.nc
    with ExitStack() as ctx:
        sb = ctx.enter_context(tc.tile_pool(name="sb", bufs=1))
        ps = ctx.enter_context(tc.psum_pool(name="ps", bufs=1))

        def tile(name, shape, dtype, tag=None):
            return sb.tile(shape, dtype, name=name, tag=tag or name, align_bytes=64)

        def load_list(name, src):
            t = tile(name, [P, S // 16], U16)
            nc.sync.dma_start(t[:], src)
            return t

        def load_words(name, src, width, tag=None):
            t = tile(name, [P, width], U32, tag)
            nc.sync.dma_start(t[:].bitcast(I32), src[0].rearrange("p c r -> p (c r)").bitcast(I32))
            return t

        def zeroed(name, width):
            t = tile(name, [P, width], U8)
            nc.vector.memset(t[:].bitcast(I32), 0)
            return t

        def load_scale_rows(queues, dst, first, src):
            for q, queue in enumerate(queues):
                queue.dma_start(dst[32 * q + first : 32 * q + first + 4, :].bitcast(I32), src[0, 4 * q : 4 * q + 4, :].bitcast(I32))

        def deal(name, src, dtype, run, tag):
            t = tile(name, [P, H], dtype, tag)
            nc.vector.tensor_copy(
                t[:].rearrange("p (t c i) -> p c t i", t=PACK, i=run),
                src[:].rearrange("p (c i t) -> p c t i", t=PACK, i=run),
            )
            return t

        def entries(lst, start, count):
            return lst[:, start // 16 : (start + count) // 16]

        def woven(t, run):
            return t[:].rearrange("p (c i t) -> p c t i", t=PACK, i=run)

        def by_runs(ap, run):
            return ap.rearrange("p t (c i) -> p c t i", i=run)

        def block(t):
            return slice(t * P, (t + 1) * P)

        def load_gain(name, src):
            t = tile(name, [P, PACK], F32)
            nc.sync.dma_start(t[:], src.rearrange("(p t) o -> p (t o)", t=PACK))
            return t

        w1s_raw = zeroed("w1s_raw", H)
        xs = zeroed("xs", T)
        xs_runs = zeroed("xs_runs", T)
        w2s_raw = zeroed("w2s_raw", H)
        w34s_raw = zeroed("w34s_raw", H)

        offs_t = load_list("offs_t", offs)
        hz_t = load_list("hz_t", hz)
        w1w_raw = load_words("w1w_raw", w1_words, H)
        xw = load_words("xw", x_words, T)
        load_scale_rows([nc.scalar, nc.scalar, nc.scalar, nc.gpsimd], w1s_raw, 0, w1_scales)
        load_scale_rows([nc.scalar] * 4, xs, 0, x_scales)
        nc.gpsimd.dma_start(xs_runs[0:P:8, :].bitcast(I32), x_scales[0].bitcast(I32))
        load_scale_rows([nc.gpsimd] * 4, w2s_raw, 0, w2_scales)
        load_scale_rows([nc.gpsimd] * 4, w34s_raw, 0, w3_scales)
        n1_t = load_list("n1_t", n1)
        gn_t = load_gain("gn_t", gn)
        n2_t = load_list("n2_t", n2)
        w2w_raw = load_words("w2w_raw", w2_words, H)
        gm_t = load_gain("gm_t", gm)
        n3_t = load_list("n3_t", n3)
        n4_t = load_list("n4_t", n4)
        n5_t = load_list("n5_t", n5)
        n6_t = load_list("n6_t", n6)
        n7_t = load_list("n7_t", n7)
        load_scale_rows([nc.sync] * 4, w34s_raw, 4, w4_scales)

        zeros = tile("zeros", [P, S], F32)
        nc.vector.memset(zeros[:], 0.0)
        y = [tile("y%d" % t, [P, 2 * S], F32) for t in range(PACK)]
        d = [tile("d%d" % t, [P, 2 * S], F32) for t in range(PACK)]
        for t in range(PACK):
            nc.scalar.activation(y[t][:, S:], zeros[:], COPY)
            nc.vector.memset(d[t][:, S:], 0.0)

        w1w = deal("w1w", w1w_raw, U32, 4, "w_words")
        xq_s = tile("xq_s", [P, S], U8)
        nc.vector.tensor_copy(xq_s[:], xs[:].indirect(offs_t[:]))
        xq_w = tile("xq_w", [P, S], U32)
        nc.vector.tensor_copy(xq_w[:], xw[:].indirect(offs_t[:]))
        w1s = deal("w1s", w1s_raw, U8, 16, "w_scales")
        xh_w = tile("xh_w", [P, S], U32)
        nc.vector.tensor_copy(xh_w[:], xw[:].indirect(hz_t[:]))

        y_ps = [ps.tile([P, S], F32, name="y_ps%d" % t, tag="bank%d" % t) for t in range(PACK)]
        for t in range(PACK):
            nc.tensor.matmul_mx(
                y_ps[t][:], lhsT=w1w[:, block(t)].bitcast(FP8X4), lhsT_scale=w1s[:, block(t)],
                rhs=xq_w[:].bitcast(FP8X4), rhs_scale=xq_s[:], start=True, stop=True,
            )
        hz_bytes = tile("hz_bytes", [P, S], U8, "xw")
        nc.vector.tensor_copy(hz_bytes[:], xs_runs[:].indirect(hz_t[:]))
        xh_s = tile("xh_s", [P, S], U8)
        nc.vector.tensor_copy(xh_s[:].bitcast(I32), hz_bytes[:].bitcast(I32))
        for r in range(1, 4):
            nc.sync.dma_start(xh_s[r:P:32, :].bitcast(I32), hz_bytes[8 * r : P : 32, :].bitcast(I32))
        w2w = deal("w2w", w2w_raw, U32, 4, "w_words")
        w2s = deal("w2s", w2s_raw, U8, 16, "w_scales")
        w4w_raw = load_words("w4w_raw", w4_words, N, "w2w_raw")
        w3w_raw = load_words("w3w_raw", w3_words, N, "w2s_raw")

        for t in range(PACK):
            nc.scalar.activation(y[t][:, :S], y_ps[t][:], COPY, scale=gn_t[:, t : t + 1])

        d_ps = [ps.tile([P, PACK, HALF], F32, name="d_ps%d" % u) for u in range(HALVES)]
        for u in range(HALVES):
            for t in range(PACK):
                nc.tensor.matmul_mx(
                    d_ps[u][:, t, :], lhsT=w2w[:, block(t)].bitcast(FP8X4), lhsT_scale=w2s[:, block(t)],
                    rhs=xh_w[:, block(u)].bitcast(FP8X4), rhs_scale=xh_s[:, block(u)], start=True, stop=True,
                )

        pa, pb, zhi, zlo, cut = [tile(name, [P, PACK, S], BF16) for name in ("pa", "pb", "zhi", "zlo", "cut")]
        for t in range(PACK):
            nc.scalar.activation(pa[:, t, :], y[t][:].indirect(n1_t[:]), COPY)
            if t < N2_ON_VECTOR:
                nc.vector.tensor_copy(pb[:, t, :], y[t][:].indirect(n2_t[:]))
            else:
                nc.scalar.activation(pb[:, t, :], y[t][:].indirect(n2_t[:]), COPY)
            if t % 2 == 1:
                g = slice(t - 1, t + 1)
                nc.vector.tensor_tensor(zhi[:, g, :], pa[:, g, :], pb[:, g, :], ALU.max)
                nc.vector.tensor_tensor(zlo[:, g, :], pa[:, g, :], pb[:, g, :], ALU.min)
                for r in (t - 1, t):
                    nc.vector.tensor_tensor(cut[:, r, :], y[r][:, :S], zhi[:, r, :], ALU.min)
        z = tile("z", [P, PACK * S], BF16)
        nc.vector.tensor_tensor(woven(z, 8), by_runs(zlo[:], 8), by_runs(cut[:], 8), ALU.max)
        z_w = tile("z_w", [P, S], U32)
        z_s = tile("z_s", [P, S], U8)
        nc.vector.quantize_mx(z_w[:].bitcast(FP8X4), z_s[:], z[:])

        for u in range(HALVES):
            for t in range(PACK):
                nc.scalar.activation(d[t][:, block(u)], d_ps[u][:, t, :], COPY, scale=gm_t[:, t : t + 1])

        w3w = deal("w3w", w3w_raw, U32, 4, "cut")
        w4w = deal("w4w", w4w_raw, U32, 4, "zlo")
        w34s = deal("w34s", w34s_raw, U8, 16, "z")

        h = y
        first_ps = [ps.tile([P, 2, HALF], F32, name="h_first%d" % u) for u in range(2)]
        last_ps = [ps.tile([P, HALF], F32, name="h_last%d" % t, tag="bank%d" % t) for t in range(PACK)]
        d3, d4 = [tile(name, [P, PACK, S], F32) for name in ("at_n3", "at_n4")]

        def fetch_d(tiles, start, count):
            cols = slice(start, start + count)
            for t in tiles:
                nc.scalar.activation(d3[:, t, cols], d[t][:].indirect(entries(n3_t, start, count)), COPY)
                nc.scalar.activation(d4[:, t, cols], d[t][:].indirect(entries(n4_t, start, count)), COPY)

        fetch_d([0, 1], 0, S)
        for u in range(HALVES):
            fetch_d([2, 3], u * HALF, HALF)
            diff = tile("diff%d" % u, [P, PACK, HALF], F32, "w34s_raw" if u == 0 else "w2s_raw")
            for g in [slice(0, 2), slice(2, 4)] if u == 0 else [slice(0, 4)]:
                nc.vector.tensor_tensor(diff[:, g, :], d3[:, g, block(u)], d4[:, g, block(u)], ALU.subtract)
            z2 = tile("z2_%d" % u, [P, PACK * HALF], BF16, "w2s_raw" if u == 0 else None)
            nc.vector.tensor_tensor(woven(z2, 4), by_runs(d_ps[u][:], 4), by_runs(diff[:], 4), ALU.mult)
            z2_w = tile("z2_w%d" % u, [P, HALF], U32, "w2w_raw" if u == 0 else None)
            z2_s = tile("z2_s%d" % u, [P, HALF], U8)
            nc.vector.quantize_mx(z2_w[:].bitcast(FP8X4), z2_s[:], z2[:])
            for t in range(PACK):
                acc = first_ps[t // 2][:, t % 2, :] if u == 0 else last_ps[t][:]
                nc.tensor.matmul_mx(
                    acc, lhsT=w3w[:, block(t)].bitcast(FP8X4), lhsT_scale=w34s[:, block(t)],
                    rhs=z_w[:, block(u)].bitcast(FP8X4), rhs_scale=z_s[:, block(u)], start=True, stop=False,
                )
                nc.tensor.matmul_mx(
                    acc, lhsT=w4w[:, block(t)].bitcast(FP8X4), lhsT_scale=w34s[4:P, block(t)],
                    rhs=z2_w[:].bitcast(FP8X4), rhs_scale=z2_s[:], start=False, stop=True,
                )
            for t in range(PACK):
                acc = first_ps[t // 2][:, t % 2, :] if u == 0 else last_ps[t][:]
                if u == 0:
                    nc.scalar.copy(h[t][:, block(u)], acc)
                else:
                    nc.vector.tensor_copy(h[t][:, block(u)], acc)

        out_w = tile("out_w", [P, S], U32)
        out_s = tile("out_s", [P, S], U8)
        out_rows = out_0.rearrange("(p t) j -> p t j", t=PACK)
        out_words = out_1[0].rearrange("p c r -> p (c r)").bitcast(I32)
        b1, b2, b3, hi, lo, up, top, mid, res = [
            tile(name, [P, PACK, S], F32) for name in ("b1", "b2", "b3", "hi", "lo", "up", "top", "mid", "res")
        ]

        def combine(tiles, start, count):
            cols = slice(start, start + count)
            for b, lst in ((b1, n5_t), (b2, n6_t), (b3, n7_t)):
                for t in tiles:
                    nc.scalar.activation(b[:, t, cols], h[t][:].indirect(entries(lst, start, count)), COPY)
            g = slice(tiles[0], tiles[-1] + 1)
            nc.vector.tensor_tensor(lo[:, g, cols], b1[:, g, cols], b2[:, g, cols], ALU.min)
            nc.vector.tensor_tensor(hi[:, g, cols], b1[:, g, cols], b2[:, g, cols], ALU.max)
            nc.vector.tensor_tensor(up[:, g, cols], lo[:, g, cols], b3[:, g, cols], ALU.max)
            nc.vector.tensor_tensor(top[:, g, cols], hi[:, g, cols], b3[:, g, cols], ALU.max)
            nc.vector.tensor_tensor(mid[:, g, cols], hi[:, g, cols], up[:, g, cols], ALU.min)
            nc.vector.scalar_tensor_tensor(res[:, g, cols], mid[:, g, cols], -0.5, top[:, g, cols], ALU.mult, ALU.add)

        combine([0], 0, S)
        combine([1], 0, S)
        nc.sync.dma_start(out_rows[:, 0:2, :], res[:, 0:2, :])
        for u in range(HALVES):
            cols = block(u)
            for tiles in [[2, 3]] if u == 0 else [[2], [3]]:
                combine(tiles, u * HALF, HALF)
            nc.sync.dma_start(out_rows[:, 2:4, cols], res[:, 2:4, cols])
            rounded = tile("rounded%d" % u, [P, PACK * HALF], BF16)
            if u == 0:
                nc.scalar.copy(woven(rounded, 4), by_runs(res[:, :, cols], 4))
            else:
                nc.vector.tensor_copy(woven(rounded, 4), by_runs(res[:, :, cols], 4))
            nc.vector.quantize_mx(out_w[:, cols].bitcast(FP8X4), out_s[:, cols], rounded[:])
            nc.sync.dma_start(out_words[:, cols], out_w[:, cols].bitcast(I32))
        for q in range(4):
            queue = nc.scalar if q < 2 else nc.sync
            queue.dma_start(out_2[0, 4 * q : 4 * q + 4, :].bitcast(I32), out_s[32 * q : 32 * q + 4, :].bitcast(I32))
